import numpy as np
import ml_dtypes


def mxq(x, axis, fmt="e4m3"):
    dtype, down = {"e4m3": (ml_dtypes.float8_e4m3fn, 7), "e5m2": (ml_dtypes.float8_e5m2, 14)}[fmt]
    v = np.moveaxis(np.asarray(x, np.float32).astype(ml_dtypes.bfloat16).astype(np.float64), axis, -1)
    blocks = v.reshape(v.shape[:-1] + (-1, 32))
    amax = np.abs(blocks).max(-1, keepdims=True)
    byte = np.maximum(np.where(amax > 0, np.frexp(amax)[1] - 1 + 127, 0) - down, 1)
    scale = np.exp2(byte - 127.0)
    codes = (blocks / scale).astype(np.float32).astype(dtype).astype(np.float64)
    return np.moveaxis((codes * scale).reshape(v.shape), -1, axis)


WIDE = False


def mx_kscale(k):
    if not WIDE:
        return np.ones(k)
    levels = np.array([10, -10, 5, -5, 0])
    if k % 512:
        return np.exp2(np.random.permutation(np.resize(levels, k // 32))).repeat(32)
    a = np.empty((k // 512, 16))
    for p in range(k // 512):
        a[p, :8] = np.random.permutation(np.resize(levels, 8))
        for g in range(8):
            far = levels[np.abs(levels - a[p, g]) >= 10]
            a[p, g + 8] = far[np.random.randint(len(far))]
    return np.exp2(a.ravel()).repeat(32)


BF16 = ml_dtypes.bfloat16


def bf(x):
    return np.asarray(x, np.float32).astype(BF16)


def f64(x):
    return np.asarray(x).astype(np.float64)

def planes(Y):
    n, m = Y.shape
    b = f64(bf(Y)).reshape(n // 32, 32, m)
    amax = np.abs(b).max(1)
    byte = np.clip(np.where(amax > 0, np.frexp(amax)[1] - 1 + 127 - 7, 1), 1, 254)
    codes = (b * np.exp2(127.0 - byte)[:, None, :]).reshape(n, m).astype(np.float32).astype(ml_dtypes.float8_e4m3fn).view(np.uint8)
    words = codes.reshape(n // 512, 128, 4, m).transpose(0, 1, 3, 2)
    return np.ascontiguousarray(words), np.ascontiguousarray(byte.astype(np.uint8).reshape(n // 512, 16, m))


T, Q, C, D = 2048, 1024, 512, 1536

BIAS = 1.0

def setup_inputs():
    s = mx_kscale(C)
    r = mx_kscale(D)
    grads = bf(np.random.randn(T, C) * s)
    feats = bf(np.random.randn(T, D) * r)
    query_grads = bf(np.random.randn(Q, C) / np.sqrt(C) / s)
    query_feats = bf(0.7 * np.random.randn(Q, D) / np.sqrt(D) / r)
    step = bf(np.exp(0.8 * np.random.randn(T)))
    query_weight = bf(1 + 0.2 * np.random.randn(Q))
    return {"grads": grads, "feats": feats, "query_grads": query_grads,
            "query_feats": query_feats, "step": step, "query_weight": query_weight}

def reference(grads, feats, query_grads, query_feats, step, query_weight):
    g = mxq(f64(grads), 1, "e4m3")
    h = mxq(f64(query_grads), 1, "e4m3")
    x = mxq(f64(feats), 1, "e4m3")
    z = mxq(f64(query_feats), 1, "e4m3")
    grad_kernel = g @ h.T
    feat_kernel = x @ z.T
    y = grad_kernel * (feat_kernel + BIAS) * f64(step)[:, None] * f64(query_weight)[None, :]
    Y = y
    words, scales = planes(Y)
    return y, words, scales

@@ -1,0 +1,271 @@
+from contextlib import ExitStack
+
+import concourse.mybir as mybir
+from concourse.masks import make_identity
+
+T, Q, C, D = 2048, 1024, 512, 1536
+FLOPS = 2 * T * Q * (C + D)
+BIAS = 1.0
+
+F32 = mybir.dt.float32
+BF16 = mybir.dt.bfloat16
+I32 = mybir.dt.int32
+U32 = mybir.dt.uint32
+U8 = mybir.dt.uint8
+FP8X4 = mybir.dt.float8_e4m3fn_x4
+MULT = mybir.AluOpType.mult
+ADD = mybir.AluOpType.add
+
+P = 128
+PACK = 4
+K_PASS = P * PACK
+PASSES = (C + D) // K_PASS
+N = 512
+HALVES = Q // N
+GROUPS = T // K_PASS
+UNITS = GROUPS * HALVES
+STEPS = UNITS * PACK
+Q_TILES = Q // P
+X_TILES = T // P
+Q_PER_HALF = N // P
+
+
+def step_of(s):
+    unit, t = divmod(s, PACK)
+    g, h = divmod(unit, HALVES)
+    return g, h, t
+
+
+def tile_gradient_feature_influence_g2_kernel(
+    tc, grads, feats, query_grads, query_feats, step, query_weight, out_0, out_1, out_2
+):
+    nc = tc.nc
+
+    with ExitStack() as ctx:
+        keep = ctx.enter_context(tc.tile_pool(name="keep", bufs=1))
+        raw = ctx.enter_context(tc.tile_pool(name="raw", bufs=Q_TILES + X_TILES))
+        xq = ctx.enter_context(tc.tile_pool(name="xq", bufs=X_TILES))
+        work = ctx.enter_context(tc.tile_pool(name="work", bufs=3))
+        turned = ctx.enter_context(tc.tile_pool(name="turned", bufs=4))
+        ps_t = ctx.enter_context(tc.psum_pool(name="ps_t", bufs=4))
+        ps_g = ctx.enter_context(tc.psum_pool(name="ps_g", bufs=2))
+        ps_f = ctx.enter_context(tc.psum_pool(name="ps_f", bufs=2))
+        ctx.enter_context(tc.manual_schedule())
+
+        ident = keep.tile([P, P], F32)
+        make_identity(nc, ident[:])
+
+        q_codes = {}
+        q_scales = {}
+        for h in range(HALVES):
+            for c in range(PASSES):
+                q_codes[h, c] = keep.tile([P, N], U32, name="q_codes_%d_%d" % (h, c), align_bytes=64)
+                q_scales[h, c] = keep.tile([P, N], U8, name="q_scales_%d_%d" % (h, c), align_bytes=64)
+        y_scales = keep.tile([P, Q], U8, align_bytes=64)
+
+        raw_tiles = {}
+        turned_tiles = {}
+        x_codes = {}
+        x_scales = {}
+        g_banks = {}
+        f_banks = {}
+        g_scaled = {}
+        y_tiles = {}
+        y_rounded = {}
+
+        def load(batch):
+            kind, n = batch
+            if kind == "q":
+                rows = slice(P * n, P * (n + 1))
+                src_g, src_f = query_grads[rows, :], query_feats[rows, :]
+            else:
+                g, t = divmod(n, PACK)
+                rows = slice(K_PASS * g + t, K_PASS * (g + 1), PACK)
+                src_g, src_f = grads[rows, :], feats[rows, :]
+            raw_g = raw.tile([P, C], BF16, align_bytes=64)
+            raw_f = raw.tile([P, D], BF16, align_bytes=64)
+            nc.sync.dma_start(out=raw_g[:], in_=src_g)
+            nc.sync.dma_start(out=raw_f[:], in_=src_f)
+            raw_tiles[batch] = (raw_g, raw_f)
+
+        def turn(batch):
+            raw_g, raw_f = raw_tiles[batch]
+            grouped = turned.tile([P, PASSES * K_PASS], BF16, align_bytes=64)
+            words_out = grouped[:].bitcast(F32)
+            for pair in range(PASSES // 2):
+                bank = ps_t.tile([P, 4, P], F32)
+                for cc in range(2):
+                    c = 2 * pair + cc
+                    if c == 0:
+                        words = raw_g[:].bitcast(F32)
+                    else:
+                        words = raw_f[:].bitcast(F32)[:, 256 * (c - 1) : 256 * c]
+                    for u in range(2):
+                        nc.tensor.transpose(bank[:, 2 * cc + u, :], words[:, u:256:2], ident[:])
+                nc.scalar.copy(
+                    out=words_out[:, 512 * pair : 512 * (pair + 1)].rearrange("p (c r u) -> p c r u", c=2, u=2),
+                    in_=bank[:].rearrange("p (c u) r -> p c r u", u=2),
+                )
+            turned_tiles[batch] = grouped
+
+        def quantize(batch):
+            kind, n = batch
+            grouped = turned_tiles[batch]
+            if kind == "q":
+                h, j = divmod(n, Q_PER_HALF)
+                cols = slice(P * j, P * (j + 1))
+                for c in range(PASSES):
+                    nc.vector.quantize_mx(
+                        out=q_codes[h, c][:, cols].bitcast(FP8X4),
+                        scales=q_scales[h, c][:, cols],
+                        in_=grouped[:, K_PASS * c : K_PASS * (c + 1)],
+                    )
+            else:
+                codes = xq.tile([P, PASSES * P], U32, align_bytes=64)
+                scales = xq.tile([P, PASSES * P], U8, align_bytes=64)
+                nc.vector.quantize_mx(out=codes[:].bitcast(FP8X4), scales=scales[:], in_=grouped[:])
+                x_codes[n], x_scales[n] = codes, scales
+
+        def mx_pass(bank, s, c, start, stop):
+            g, h, t = step_of(s)
+            n = PACK * g + t
+            cols = slice(P * c, P * (c + 1))
+            nc.tensor.matmul_mx(
+                out=bank[:],
+                lhsT=x_codes[n][:, cols].bitcast(FP8X4),
+                lhsT_scale=x_scales[n][:, cols],
+                rhs=q_codes[h, c][:].bitcast(FP8X4),
+                rhs_scale=q_scales[h, c][:],
+                start=start,
+                stop=stop,
+            )
+
+        def grad_matmul(s):
+            g_bank = ps_g.tile([P, N], F32)
+            mx_pass(g_bank, s, 0, True, True)
+            g_banks[s] = g_bank
+
+        def feat_matmul(s):
+            f_bank = ps_f.tile([P, N], F32)
+            for c in range(1, PASSES):
+                mx_pass(f_bank, s, c, c == 1, c == PASSES - 1)
+            f_banks[s] = f_bank
+
+        def scale_grad(s):
+            g, h, t = step_of(s)
+            n = PACK * g + t
+            scaled = work.tile([P, N], F32)
+            nc.vector.scalar_tensor_tensor(
+                out=scaled[:], in0=g_banks[s][:], scalar=step_f32[:, n : n + 1],
+                in1=weight_rows[:, N * h : N * (h + 1)], op0=MULT, op1=MULT,
+            )
+            g_scaled[s] = scaled
+
+        def finish(s):
+            g, h, t = step_of(s)
+            unit = s // PACK
+            if t == 0:
+                y_unit = work.tile([P, PACK, N], F32)
+                y_tiles[unit] = y_unit
+            y_t = y_tiles[unit][:, t, :]
+            nc.vector.scalar_tensor_tensor(
+                out=y_t, in0=f_banks[s][:], scalar=BIAS, in1=g_scaled[s][:], op0=ADD, op1=MULT,
+            )
+            nc.sync.dma_start(
+                out=out_0[K_PASS * g + t : K_PASS * (g + 1) : PACK, N * h : N * (h + 1)], in_=y_t
+            )
+
+        def round_unit(unit):
+            rounded = work.tile([P, N * PACK], BF16, align_bytes=64)
+            nc.scalar.copy(
+                out=rounded[:].rearrange("p (c i t) -> p c t i", i=4, t=PACK),
+                in_=y_tiles[unit][:].rearrange("p t (c i) -> p c t i", i=4),
+            )
+            y_rounded[unit] = rounded
+
+        def quantize_unit(unit):
+            g, h = divmod(unit, HALVES)
+            y_words = work.tile([P, N], U32, align_bytes=64)
+            nc.vector.quantize_mx(
+                out=y_words[:].bitcast(FP8X4),
+                scales=y_scales[4 * g : P, N * h : N * (h + 1)],
+                in_=y_rounded[unit][:],
+            )
+            nc.sync.dma_start(
+                out=out_1[g].rearrange("p m t -> p (m t)")[:, PACK * N * h : PACK * N * (h + 1)].bitcast(I32),
+                in_=y_words[:].bitcast(I32),
+            )
+
+        head = [("q", 0), ("q", 1), ("q", 2), ("q", 3), ("x", 0), ("x", 1)]
+        runs = {
+            0: [("x", 2), ("q", 4)],
+            1: [("x", 3), ("q", 5)],
+            2: [("q", 6), ("q", 7)],
+            3: [("x", 4), ("x", 5)],
+        }
+        for i in range(5):
+            runs[8 + 4 * i] = [("x", 6 + 2 * i), ("x", 7 + 2 * i)]
+
+        load(head[0])
+        weight_cols = keep.tile([P, Q // P], BF16)
+        nc.sync.dma_start(out=weight_cols[:], in_=query_weight.rearrange("(p c) -> p c", p=P))
+        step_bf = keep.tile([P, GROUPS, PACK], BF16)
+        nc.sync.dma_start(out=step_bf[:], in_=step.rearrange("(g p t) -> p g t", g=GROUPS, t=PACK))
+        for batch in head[1:] + runs[0] + runs[1] + runs[2] + runs[3]:
+            load(batch)
+
+        step_f32 = keep.tile([P, X_TILES], F32)
+        nc.vector.tensor_copy(out=step_f32[:], in_=step_bf[:].rearrange("p g t -> p (g t)"))
+
+        turn(head[0])
+        weight_rows = keep.tile([P, Q], BF16)
+        weight_bank = ps_t.tile([P, 4, P], F32, name="bank")
+        for c in range(4):
+            nc.tensor.transpose(
+                weight_bank[:, c, :],
+                weight_cols[:].bitcast(F32)[:, c : c + 1].to_broadcast([P, P]),
+                ident[:],
+            )
+        nc.vector.tensor_copy(
+            out=weight_rows[:].bitcast(F32).rearrange("p (n c) -> p n c", c=4),
+            in_=weight_bank[:].rearrange("p c n -> p n c"),
+        )
+        quantize(head[0])
+        for batch in head[1:]:
+            turn(batch)
+            quantize(batch)
+
+        for s in range(STEPS):
+            run = runs.get(s, [])
+            for batch in run:
+                turn(batch)
+            unit = s // PACK
+            if s % PACK == 0 and unit >= 1:
+                round_unit(unit - 1)
+            if s % PACK == 0 and unit >= 2:
+                quantize_unit(unit - 2)
+            if s == 0:
+                grad_matmul(0)
+                scale_grad(0)
+            if run:
+                quantize(run[0])
+            if s + 1 < STEPS:
+                grad_matmul(s + 1)
+            feat_matmul(s)
+            if s + 1 < STEPS:
+                scale_grad(s + 1)
+            if run:
+                quantize(run[1])
+            if s == STEPS - 1:
+                quantize_unit(UNITS - 2)
+            finish(s)
+            if 1 <= s <= 10:
+                load(("x", 5 + s))
+
+        round_unit(UNITS - 1)
+        quantize_unit(UNITS - 1)
+        for quad in range(4):
+            nc.sync.dma_start(
+                out=out_2[:, 4 * quad : 4 * quad + 4, :].bitcast(I32),
+                in_=y_scales[32 * quad : 32 * quad + 16, :].bitcast(I32),
+            )

@@ -20,20 +20,35 @@ P = 128
 PACK = 4
 K_PASS = P * PACK
 PASSES = (C + D) // K_PASS
+ROW_PAIRS = (C + D) // 2
+PASS_PAIRS = K_PASS // 2
 N = 512
 HALVES = Q // N
 GROUPS = T // K_PASS
 UNITS = GROUPS * HALVES
 STEPS = UNITS * PACK
-Q_TILES = Q // P
-X_TILES = T // P
-Q_PER_HALF = N // P
+SAMPLE_TILES = T // P
+QUERY_TILES_A_HALF = N // P
+LINE = 4
+
+FIRST_UNIT_SORTED = 2
+LATER_SORTED = 3
+LONE_RUN_STEP = 6
+LAST_VECTOR_COLUMNS = 352
 
 
-def step_of(s):
+def place_of(s):
     unit, t = divmod(s, PACK)
     g, h = divmod(unit, HALVES)
     return g, h, t
+
+
+def samples(n):
+    return ("samples", n)
+
+
+def queries(n):
+    return ("queries", n)
 
 
 def tile_gradient_feature_influence_g2_kernel(
@@ -43,229 +58,271 @@ def tile_gradient_feature_influence_g2_kernel(
 
     with ExitStack() as ctx:
         keep = ctx.enter_context(tc.tile_pool(name="keep", bufs=1))
-        raw = ctx.enter_context(tc.tile_pool(name="raw", bufs=Q_TILES + X_TILES))
-        xq = ctx.enter_context(tc.tile_pool(name="xq", bufs=X_TILES))
+        raw = ctx.enter_context(tc.tile_pool(name="raw", bufs=20))
+        sorter = ctx.enter_context(tc.tile_pool(name="sorter", bufs=3))
+        sample_mx = ctx.enter_context(tc.tile_pool(name="sample_mx", bufs=SAMPLE_TILES))
         work = ctx.enter_context(tc.tile_pool(name="work", bufs=3))
         turned = ctx.enter_context(tc.tile_pool(name="turned", bufs=4))
-        ps_t = ctx.enter_context(tc.psum_pool(name="ps_t", bufs=4))
-        ps_g = ctx.enter_context(tc.psum_pool(name="ps_g", bufs=2))
-        ps_f = ctx.enter_context(tc.psum_pool(name="ps_f", bufs=2))
+        ps_turn = ctx.enter_context(tc.psum_pool(name="ps_turn", bufs=4))
+        ps_grad = ctx.enter_context(tc.psum_pool(name="ps_grad", bufs=2))
+        ps_feat = ctx.enter_context(tc.psum_pool(name="ps_feat", bufs=2))
         ctx.enter_context(tc.manual_schedule())
 
         ident = keep.tile([P, P], F32)
         make_identity(nc, ident[:])
 
-        q_codes = {}
-        q_scales = {}
+        query_codes = {}
+        query_scales = {}
         for h in range(HALVES):
             for c in range(PASSES):
-                q_codes[h, c] = keep.tile([P, N], U32, name="q_codes_%d_%d" % (h, c), align_bytes=64)
-                q_scales[h, c] = keep.tile([P, N], U8, name="q_scales_%d_%d" % (h, c), align_bytes=64)
+                query_codes[h, c] = keep.tile([P, N], U32, name="query_codes_%d_%d" % (h, c), align_bytes=64)
+                query_scales[h, c] = keep.tile([P, N], U8, name="query_scales_%d_%d" % (h, c), align_bytes=64)
         y_scales = keep.tile([P, Q], U8, align_bytes=64)
 
         raw_tiles = {}
+        sorted_tiles = {}
         turned_tiles = {}
-        x_codes = {}
-        x_scales = {}
-        g_banks = {}
-        f_banks = {}
-        g_scaled = {}
+        sample_codes = {}
+        sample_scales = {}
+        grad_banks = {}
+        feat_banks = {}
+        weighted_grads = {}
         y_tiles = {}
-        y_rounded = {}
+        rounded_tiles = {}
 
-        def load(batch):
-            kind, n = batch
-            if kind == "q":
+        def load(row_tile):
+            kind, n = row_tile
+            if kind == "queries":
                 rows = slice(P * n, P * (n + 1))
-                src_g, src_f = query_grads[rows, :], query_feats[rows, :]
+                grad_rows, feat_rows = query_grads[rows, :], query_feats[rows, :]
             else:
                 g, t = divmod(n, PACK)
                 rows = slice(K_PASS * g + t, K_PASS * (g + 1), PACK)
-                src_g, src_f = grads[rows, :], feats[rows, :]
-            raw_g = raw.tile([P, C], BF16, align_bytes=64)
-            raw_f = raw.tile([P, D], BF16, align_bytes=64)
-            nc.sync.dma_start(out=raw_g[:], in_=src_g)
-            nc.sync.dma_start(out=raw_f[:], in_=src_f)
-            raw_tiles[batch] = (raw_g, raw_f)
+                grad_rows, feat_rows = grads[rows, :], feats[rows, :]
+            raw_pairs = raw.tile([P, ROW_PAIRS], F32, align_bytes=64)
+            nc.sync.dma_start(out=raw_pairs[:, : C // 2], in_=grad_rows.bitcast(F32))
+            nc.sync.dma_start(out=raw_pairs[:, C // 2 :], in_=feat_rows.bitcast(F32))
+            raw_tiles[row_tile] = raw_pairs
 
-        def turn(batch):
-            raw_g, raw_f = raw_tiles[batch]
+        def sort_pairs(row_tile, copy, passes):
+            sorted_pairs = sorter.tile([P, 2, P * passes], F32, align_bytes=64)
+            copy(
+                out=sorted_pairs[:],
+                in_=raw_tiles[row_tile][:, ROW_PAIRS - PASS_PAIRS * passes :].rearrange("p (w u) -> p u w", u=2),
+            )
+            sorted_tiles[row_tile] = (sorted_pairs, PASSES - passes)
+
+        def turn(row_tile):
             grouped = turned.tile([P, PASSES * K_PASS], BF16, align_bytes=64)
-            words_out = grouped[:].bitcast(F32)
-            for pair in range(PASSES // 2):
-                bank = ps_t.tile([P, 4, P], F32)
-                for cc in range(2):
-                    c = 2 * pair + cc
-                    if c == 0:
-                        words = raw_g[:].bitcast(F32)
-                    else:
-                        words = raw_f[:].bitcast(F32)[:, 256 * (c - 1) : 256 * c]
+            grouped_pairs = grouped[:].bitcast(F32)
+            sorted_pairs, first_sorted = sorted_tiles.get(row_tile, (None, PASSES))
+            for c0 in range(0, PASSES, 2):
+                bank = ps_turn.tile([P, 4, P], F32)
+                for c in (c0, c0 + 1):
                     for u in range(2):
-                        nc.tensor.transpose(bank[:, 2 * cc + u, :], words[:, u:256:2], ident[:])
+                        if c >= first_sorted:
+                            pairs = sorted_pairs[:, u, P * (c - first_sorted) : P * (c - first_sorted + 1)]
+                        else:
+                            pairs = raw_tiles[row_tile][:, PASS_PAIRS * c + u : PASS_PAIRS * (c + 1) : 2]
+                        nc.tensor.transpose(bank[:, 2 * (c - c0) + u, :], pairs, ident[:])
                 nc.scalar.copy(
-                    out=words_out[:, 512 * pair : 512 * (pair + 1)].rearrange("p (c r u) -> p c r u", c=2, u=2),
+                    out=grouped_pairs[:, PASS_PAIRS * c0 : PASS_PAIRS * (c0 + 2)].rearrange(
+                        "p (c r u) -> p c r u", c=2, u=2
+                    ),
                     in_=bank[:].rearrange("p (c u) r -> p c r u", u=2),
                 )
-            turned_tiles[batch] = grouped
+            turned_tiles[row_tile] = grouped
 
-        def quantize(batch):
-            kind, n = batch
-            grouped = turned_tiles[batch]
-            if kind == "q":
-                h, j = divmod(n, Q_PER_HALF)
+        def quantize(row_tile):
+            kind, n = row_tile
+            grouped = turned_tiles[row_tile]
+            if kind == "queries":
+                h, j = divmod(n, QUERY_TILES_A_HALF)
                 cols = slice(P * j, P * (j + 1))
                 for c in range(PASSES):
                     nc.vector.quantize_mx(
-                        out=q_codes[h, c][:, cols].bitcast(FP8X4),
-                        scales=q_scales[h, c][:, cols],
+                        out=query_codes[h, c][:, cols].bitcast(FP8X4),
+                        scales=query_scales[h, c][:, cols],
                         in_=grouped[:, K_PASS * c : K_PASS * (c + 1)],
                     )
             else:
-                codes = xq.tile([P, PASSES * P], U32, align_bytes=64)
-                scales = xq.tile([P, PASSES * P], U8, align_bytes=64)
+                codes = sample_mx.tile([P, PASSES * P], U32, align_bytes=64)
+                scales = sample_mx.tile([P, PASSES * P], U8, align_bytes=64)
                 nc.vector.quantize_mx(out=codes[:].bitcast(FP8X4), scales=scales[:], in_=grouped[:])
-                x_codes[n], x_scales[n] = codes, scales
+                sample_codes[n], sample_scales[n] = codes, scales
 
         def mx_pass(bank, s, c, start, stop):
-            g, h, t = step_of(s)
-            n = PACK * g + t
+            g, h, t = place_of(s)
             cols = slice(P * c, P * (c + 1))
             nc.tensor.matmul_mx(
                 out=bank[:],
-                lhsT=x_codes[n][:, cols].bitcast(FP8X4),
-                lhsT_scale=x_scales[n][:, cols],
-                rhs=q_codes[h, c][:].bitcast(FP8X4),
-                rhs_scale=q_scales[h, c][:],
+                lhsT=sample_codes[PACK * g + t][:, cols].bitcast(FP8X4),
+                lhsT_scale=sample_scales[PACK * g + t][:, cols],
+                rhs=query_codes[h, c][:].bitcast(FP8X4),
+                rhs_scale=query_scales[h, c][:],
                 start=start,
                 stop=stop,
             )
 
         def grad_matmul(s):
-            g_bank = ps_g.tile([P, N], F32)
-            mx_pass(g_bank, s, 0, True, True)
-            g_banks[s] = g_bank
+            grad_bank = ps_grad.tile([P, N], F32)
+            mx_pass(grad_bank, s, 0, True, True)
+            grad_banks[s] = grad_bank
 
         def feat_matmul(s):
-            f_bank = ps_f.tile([P, N], F32)
+            feat_bank = ps_feat.tile([P, N], F32)
             for c in range(1, PASSES):
-                mx_pass(f_bank, s, c, c == 1, c == PASSES - 1)
-            f_banks[s] = f_bank
+                mx_pass(feat_bank, s, c, c == 1, c == PASSES - 1)
+            feat_banks[s] = feat_bank
 
-        def scale_grad(s):
-            g, h, t = step_of(s)
+        def weigh_grad(s):
+            g, h, t = place_of(s)
             n = PACK * g + t
-            scaled = work.tile([P, N], F32)
+            weighted = work.tile([P, N], F32, bufs=4)
             nc.vector.scalar_tensor_tensor(
-                out=scaled[:], in0=g_banks[s][:], scalar=step_f32[:, n : n + 1],
-                in1=weight_rows[:, N * h : N * (h + 1)], op0=MULT, op1=MULT,
+                out=weighted[:],
+                in0=grad_banks[s][:],
+                scalar=step_cols[:, n : n + 1],
+                in1=weight_rows[:, N * h : N * (h + 1)],
+                op0=MULT,
+                op1=MULT,
             )
-            g_scaled[s] = scaled
+            weighted_grads[s] = weighted
 
         def finish(s):
-            g, h, t = step_of(s)
+            g, h, t = place_of(s)
             unit = s // PACK
             if t == 0:
                 y_unit = work.tile([P, PACK, N], F32)
                 y_tiles[unit] = y_unit
-            y_t = y_tiles[unit][:, t, :]
+            y_step = y_tiles[unit][:, t, :]
             nc.vector.scalar_tensor_tensor(
-                out=y_t, in0=f_banks[s][:], scalar=BIAS, in1=g_scaled[s][:], op0=ADD, op1=MULT,
+                out=y_step, in0=feat_banks[s][:], scalar=BIAS, in1=weighted_grads[s][:], op0=ADD, op1=MULT
             )
             nc.sync.dma_start(
-                out=out_0[K_PASS * g + t : K_PASS * (g + 1) : PACK, N * h : N * (h + 1)], in_=y_t
+                out=out_0[K_PASS * g + t : K_PASS * (g + 1) : PACK, N * h : N * (h + 1)], in_=y_step
             )
 
-        def round_unit(unit):
+        def round_unit(unit, shares):
             rounded = work.tile([P, N * PACK], BF16, align_bytes=64)
-            nc.scalar.copy(
-                out=rounded[:].rearrange("p (c i t) -> p c t i", i=4, t=PACK),
-                in_=y_tiles[unit][:].rearrange("p t (c i) -> p c t i", i=4),
-            )
-            y_rounded[unit] = rounded
+            for copy, first, last in shares:
+                copy(
+                    out=rounded[:, PACK * first : PACK * last].rearrange("p (c i t) -> p c t i", i=LINE, t=PACK),
+                    in_=y_tiles[unit][:, :, first:last].rearrange("p t (c i) -> p c t i", i=LINE),
+                )
+            rounded_tiles[unit] = rounded
 
         def quantize_unit(unit):
             g, h = divmod(unit, HALVES)
-            y_words = work.tile([P, N], U32, align_bytes=64)
+            y_codes = work.tile([P, N], U32, align_bytes=64)
             nc.vector.quantize_mx(
-                out=y_words[:].bitcast(FP8X4),
+                out=y_codes[:].bitcast(FP8X4),
                 scales=y_scales[4 * g : P, N * h : N * (h + 1)],
-                in_=y_rounded[unit][:],
+                in_=rounded_tiles[unit][:],
             )
             nc.sync.dma_start(
                 out=out_1[g].rearrange("p m t -> p (m t)")[:, PACK * N * h : PACK * N * (h + 1)].bitcast(I32),
-                in_=y_words[:].bitcast(I32),
+                in_=y_codes[:].bitcast(I32),
             )
 
-        head = [("q", 0), ("q", 1), ("q", 2), ("q", 3), ("x", 0), ("x", 1)]
-        runs = {
-            0: [("x", 2), ("q", 4)],
-            1: [("x", 3), ("q", 5)],
-            2: [("q", 6), ("q", 7)],
-            3: [("x", 4), ("x", 5)],
-        }
-        for i in range(5):
-            runs[8 + 4 * i] = [("x", 6 + 2 * i), ("x", 7 + 2 * i)]
+        head = [samples(0)] + [queries(j) for j in range(QUERY_TILES_A_HALF)] + [samples(1)]
+        first_runs = [
+            [samples(2), queries(4)],
+            [samples(3), queries(5)],
+            [queries(6), queries(7)],
+            [samples(4), samples(5)],
+        ]
+        lone = first_runs[-1][-1][1] + 1
+        later_runs = {LONE_RUN_STEP: [samples(lone)]}
+        for i, n in enumerate(range(lone + 1, SAMPLE_TILES, 2)):
+            later_runs[PACK * (2 + i)] = [samples(m) for m in range(n, min(n + 2, SAMPLE_TILES))]
+        run_steps = sorted(later_runs)
 
-        load(head[0])
+        for row_tile in head:
+            load(row_tile)
         weight_cols = keep.tile([P, Q // P], BF16)
         nc.sync.dma_start(out=weight_cols[:], in_=query_weight.rearrange("(p c) -> p c", p=P))
-        step_bf = keep.tile([P, GROUPS, PACK], BF16)
-        nc.sync.dma_start(out=step_bf[:], in_=step.rearrange("(g p t) -> p g t", g=GROUPS, t=PACK))
-        for batch in head[1:] + runs[0] + runs[1] + runs[2] + runs[3]:
-            load(batch)
+        step_bf16 = keep.tile([P, GROUPS, PACK], BF16)
+        nc.sync.dma_start(out=step_bf16[:], in_=step.rearrange("(g p t) -> p g t", g=GROUPS, t=PACK))
+        for run in first_runs + [later_runs[LONE_RUN_STEP]]:
+            for row_tile in run:
+                load(row_tile)
 
-        step_f32 = keep.tile([P, X_TILES], F32)
-        nc.vector.tensor_copy(out=step_f32[:], in_=step_bf[:].rearrange("p g t -> p (g t)"))
+        def load_behind(s):
+            if s >= 1 and lone + s < SAMPLE_TILES:
+                load(samples(lone + s))
 
         turn(head[0])
-        weight_rows = keep.tile([P, Q], BF16)
-        weight_bank = ps_t.tile([P, 4, P], F32, name="bank")
-        for c in range(4):
-            nc.tensor.transpose(
-                weight_bank[:, c, :],
-                weight_cols[:].bitcast(F32)[:, c : c + 1].to_broadcast([P, P]),
-                ident[:],
-            )
-        nc.vector.tensor_copy(
-            out=weight_rows[:].bitcast(F32).rearrange("p (n c) -> p n c", c=4),
-            in_=weight_bank[:].rearrange("p c n -> p n c"),
-        )
-        quantize(head[0])
-        for batch in head[1:]:
-            turn(batch)
-            quantize(batch)
+        for i in range(1, len(head)):
+            turn(head[i])
+            quantize(head[i - 1])
 
-        for s in range(STEPS):
-            run = runs.get(s, [])
-            for batch in run:
-                turn(batch)
-            unit = s // PACK
-            if s % PACK == 0 and unit >= 1:
-                round_unit(unit - 1)
-            if s % PACK == 0 and unit >= 2:
-                quantize_unit(unit - 2)
-            if s == 0:
-                grad_matmul(0)
-                scale_grad(0)
-            if run:
-                quantize(run[0])
+        step_cols = keep.tile([P, SAMPLE_TILES], F32)
+        weight_rows = keep.tile([P, Q], BF16)
+        bank = ps_turn.tile([P, 4, P], F32)
+        for i in range(4):
+            nc.tensor.transpose(
+                bank[:, i, :], weight_cols[:].bitcast(F32)[:, i : i + 1].to_broadcast([P, P]), ident[:]
+            )
+        nc.vector.tensor_copy(out=step_cols[:], in_=step_bf16[:].rearrange("p g t -> p (g t)"))
+        nc.vector.tensor_copy(
+            out=weight_rows[:].bitcast(F32).rearrange("p (n i) -> p n i", i=4),
+            in_=bank[:].rearrange("p i n -> p n i"),
+        )
+
+        sort_pairs(first_runs[0][0], nc.vector.tensor_copy, FIRST_UNIT_SORTED)
+        waiting = head[-1:]
+        for s in range(PACK):
+            grad_matmul(s)
+            weigh_grad(s)
+            quantize(waiting[0])
+            feat_matmul(s)
+            finish(s)
+            for row_tile in waiting[1:]:
+                quantize(row_tile)
+            sort_pairs(first_runs[s][1], nc.scalar.copy, FIRST_UNIT_SORTED)
+            if s + 1 < PACK:
+                sort_pairs(first_runs[s + 1][0], nc.vector.tensor_copy, FIRST_UNIT_SORTED)
+            load_behind(s)
+            waiting = first_runs[s]
+            for row_tile in waiting:
+                turn(row_tile)
+
+        grad_matmul(PACK)
+        weigh_grad(PACK)
+        for s in range(PACK, STEPS):
+            unit, t = divmod(s, PACK)
+            due = [samples(n) for n in (2 * unit + 2, 2 * unit + 3) if t == 0 and n < SAMPLE_TILES]
             if s + 1 < STEPS:
                 grad_matmul(s + 1)
+            for row_tile in later_runs.get(s, []):
+                turn(row_tile)
+            if t == 0 and unit >= 2:
+                quantize_unit(unit - 2)
+            for row_tile in due[:1]:
+                quantize(row_tile)
             feat_matmul(s)
             if s + 1 < STEPS:
-                scale_grad(s + 1)
-            if run:
-                quantize(run[1])
-            if s == STEPS - 1:
+                weigh_grad(s + 1)
+            else:
                 quantize_unit(UNITS - 2)
+            for row_tile in due[1:]:
+                quantize(row_tile)
+            if t == 0:
+                round_unit(unit - 1, [(nc.scalar.copy, 0, N)])
             finish(s)
-            if 1 <= s <= 10:
-                load(("x", 5 + s))
+            if s in run_steps[:-1]:
+                for row_tile in later_runs[run_steps[run_steps.index(s) + 1]][1:]:
+                    sort_pairs(row_tile, nc.scalar.copy, LATER_SORTED)
+            load_behind(s)
 
-        round_unit(UNITS - 1)
+        round_unit(
+            UNITS - 1,
+            [(nc.vector.tensor_copy, 0, LAST_VECTOR_COLUMNS), (nc.scalar.copy, LAST_VECTOR_COLUMNS, N)],
+        )
         quantize_unit(UNITS - 1)
-        for quad in range(4):
-            nc.sync.dma_start(
-                out=out_2[:, 4 * quad : 4 * quad + 4, :].bitcast(I32),
-                in_=y_scales[32 * quad : 32 * quad + 16, :].bitcast(I32),
+        for quadrant in range(4):
+            nc.scalar.dma_start(
+                out=out_2[:, 4 * quadrant : 4 * quadrant + 4, :].bitcast(I32),
+                in_=y_scales[32 * quadrant : 32 * quadrant + 16, :].bitcast(I32),
             )

from contextlib import ExitStack

import concourse.mybir as mybir
from concourse.masks import make_identity

T, Q, C, D = 2048, 1024, 512, 1536
FLOPS = 2 * T * Q * (C + D)
BIAS = 1.0

F32 = mybir.dt.float32
BF16 = mybir.dt.bfloat16
I32 = mybir.dt.int32
U32 = mybir.dt.uint32
U8 = mybir.dt.uint8
FP8X4 = mybir.dt.float8_e4m3fn_x4
MULT = mybir.AluOpType.mult
ADD = mybir.AluOpType.add

P = 128
PACK = 4
K_PASS = P * PACK
PASSES = (C + D) // K_PASS
ROW_PAIRS = (C + D) // 2
PASS_PAIRS = K_PASS // 2
N = 512
HALVES = Q // N
GROUPS = T // K_PASS
UNITS = GROUPS * HALVES
STEPS = UNITS * PACK
SAMPLE_TILES = T // P
QUERY_TILES_A_HALF = N // P
LINE = 4

FIRST_UNIT_SORTED = 2
LATER_SORTED = 3
LONE_RUN_STEP = 6
LAST_VECTOR_COLUMNS = 352


def place_of(s):
    unit, t = divmod(s, PACK)
    g, h = divmod(unit, HALVES)
    return g, h, t


def samples(n):
    return ("samples", n)


def queries(n):
    return ("queries", n)


def tile_gradient_feature_influence_g2_kernel(
    tc, grads, feats, query_grads, query_feats, step, query_weight, out_0, out_1, out_2
):
    nc = tc.nc

    with ExitStack() as ctx:
        keep = ctx.enter_context(tc.tile_pool(name="keep", bufs=1))
        raw = ctx.enter_context(tc.tile_pool(name="raw", bufs=20))
        sorter = ctx.enter_context(tc.tile_pool(name="sorter", bufs=3))
        sample_mx = ctx.enter_context(tc.tile_pool(name="sample_mx", bufs=SAMPLE_TILES))
        work = ctx.enter_context(tc.tile_pool(name="work", bufs=3))
        turned = ctx.enter_context(tc.tile_pool(name="turned", bufs=4))
        ps_turn = ctx.enter_context(tc.psum_pool(name="ps_turn", bufs=4))
        ps_grad = ctx.enter_context(tc.psum_pool(name="ps_grad", bufs=2))
        ps_feat = ctx.enter_context(tc.psum_pool(name="ps_feat", bufs=2))
        ctx.enter_context(tc.manual_schedule())

        ident = keep.tile([P, P], F32)
        make_identity(nc, ident[:])

        query_codes = {}
        query_scales = {}
        for h in range(HALVES):
            for c in range(PASSES):
                query_codes[h, c] = keep.tile([P, N], U32, name="query_codes_%d_%d" % (h, c), align_bytes=64)
                query_scales[h, c] = keep.tile([P, N], U8, name="query_scales_%d_%d" % (h, c), align_bytes=64)
        y_scales = keep.tile([P, Q], U8, align_bytes=64)

        raw_tiles = {}
        sorted_tiles = {}
        turned_tiles = {}
        sample_codes = {}
        sample_scales = {}
        grad_banks = {}
        feat_banks = {}
        weighted_grads = {}
        y_tiles = {}
        rounded_tiles = {}

        def load(row_tile):
            kind, n = row_tile
            if kind == "queries":
                rows = slice(P * n, P * (n + 1))
                grad_rows, feat_rows = query_grads[rows, :], query_feats[rows, :]
            else:
                g, t = divmod(n, PACK)
                rows = slice(K_PASS * g + t, K_PASS * (g + 1), PACK)
                grad_rows, feat_rows = grads[rows, :], feats[rows, :]
            raw_pairs = raw.tile([P, ROW_PAIRS], F32, align_bytes=64)
            nc.sync.dma_start(out=raw_pairs[:, : C // 2], in_=grad_rows.bitcast(F32))
            nc.sync.dma_start(out=raw_pairs[:, C // 2 :], in_=feat_rows.bitcast(F32))
            raw_tiles[row_tile] = raw_pairs

        def sort_pairs(row_tile, copy, passes):
            sorted_pairs = sorter.tile([P, 2, P * passes], F32, align_bytes=64)
            copy(
                out=sorted_pairs[:],
                in_=raw_tiles[row_tile][:, ROW_PAIRS - PASS_PAIRS * passes :].rearrange("p (w u) -> p u w", u=2),
            )
            sorted_tiles[row_tile] = (sorted_pairs, PASSES - passes)

        def turn(row_tile):
            grouped = turned.tile([P, PASSES * K_PASS], BF16, align_bytes=64)
            grouped_pairs = grouped[:].bitcast(F32)
            sorted_pairs, first_sorted = sorted_tiles.get(row_tile, (None, PASSES))
            for c0 in range(0, PASSES, 2):
                bank = ps_turn.tile([P, 4, P], F32)
                for c in (c0, c0 + 1):
                    for u in range(2):
                        if c >= first_sorted:
                            pairs = sorted_pairs[:, u, P * (c - first_sorted) : P * (c - first_sorted + 1)]
                        else:
                            pairs = raw_tiles[row_tile][:, PASS_PAIRS * c + u : PASS_PAIRS * (c + 1) : 2]
                        nc.tensor.transpose(bank[:, 2 * (c - c0) + u, :], pairs, ident[:])
                nc.scalar.copy(
                    out=grouped_pairs[:, PASS_PAIRS * c0 : PASS_PAIRS * (c0 + 2)].rearrange(
                        "p (c r u) -> p c r u", c=2, u=2
                    ),
                    in_=bank[:].rearrange("p (c u) r -> p c r u", u=2),
                )
            turned_tiles[row_tile] = grouped

        def quantize(row_tile):
            kind, n = row_tile
            grouped = turned_tiles[row_tile]
            if kind == "queries":
                h, j = divmod(n, QUERY_TILES_A_HALF)
                cols = slice(P * j, P * (j + 1))
                for c in range(PASSES):
                    nc.vector.quantize_mx(
                        out=query_codes[h, c][:, cols].bitcast(FP8X4),
                        scales=query_scales[h, c][:, cols],
                        in_=grouped[:, K_PASS * c : K_PASS * (c + 1)],
                    )
            else:
                codes = sample_mx.tile([P, PASSES * P], U32, align_bytes=64)
                scales = sample_mx.tile([P, PASSES * P], U8, align_bytes=64)
                nc.vector.quantize_mx(out=codes[:].bitcast(FP8X4), scales=scales[:], in_=grouped[:])
                sample_codes[n], sample_scales[n] = codes, scales

        def mx_pass(bank, s, c, start, stop):
            g, h, t = place_of(s)
            cols = slice(P * c, P * (c + 1))
            nc.tensor.matmul_mx(
                out=bank[:],
                lhsT=sample_codes[PACK * g + t][:, cols].bitcast(FP8X4),
                lhsT_scale=sample_scales[PACK * g + t][:, cols],
                rhs=query_codes[h, c][:].bitcast(FP8X4),
                rhs_scale=query_scales[h, c][:],
                start=start,
                stop=stop,
            )

        def grad_matmul(s):
            grad_bank = ps_grad.tile([P, N], F32)
            mx_pass(grad_bank, s, 0, True, True)
            grad_banks[s] = grad_bank

        def feat_matmul(s):
            feat_bank = ps_feat.tile([P, N], F32)
            for c in range(1, PASSES):
                mx_pass(feat_bank, s, c, c == 1, c == PASSES - 1)
            feat_banks[s] = feat_bank

        def weigh_grad(s):
            g, h, t = place_of(s)
            n = PACK * g + t
            weighted = work.tile([P, N], F32, bufs=4)
            nc.vector.scalar_tensor_tensor(
                out=weighted[:],
                in0=grad_banks[s][:],
                scalar=step_cols[:, n : n + 1],
                in1=weight_rows[:, N * h : N * (h + 1)],
                op0=MULT,
                op1=MULT,
            )
            weighted_grads[s] = weighted

        def finish(s):
            g, h, t = place_of(s)
            unit = s // PACK
            if t == 0:
                y_unit = work.tile([P, PACK, N], F32)
                y_tiles[unit] = y_unit
            y_step = y_tiles[unit][:, t, :]
            nc.vector.scalar_tensor_tensor(
                out=y_step, in0=feat_banks[s][:], scalar=BIAS, in1=weighted_grads[s][:], op0=ADD, op1=MULT
            )
            nc.sync.dma_start(
                out=out_0[K_PASS * g + t : K_PASS * (g + 1) : PACK, N * h : N * (h + 1)], in_=y_step
            )

        def round_unit(unit, shares):
            rounded = work.tile([P, N * PACK], BF16, align_bytes=64)
            for copy, first, last in shares:
                copy(
                    out=rounded[:, PACK * first : PACK * last].rearrange("p (c i t) -> p c t i", i=LINE, t=PACK),
                    in_=y_tiles[unit][:, :, first:last].rearrange("p t (c i) -> p c t i", i=LINE),
                )
            rounded_tiles[unit] = rounded

        def quantize_unit(unit):
            g, h = divmod(unit, HALVES)
            y_codes = work.tile([P, N], U32, align_bytes=64)
            nc.vector.quantize_mx(
                out=y_codes[:].bitcast(FP8X4),
                scales=y_scales[4 * g : P, N * h : N * (h + 1)],
                in_=rounded_tiles[unit][:],
            )
            nc.sync.dma_start(
                out=out_1[g].rearrange("p m t -> p (m t)")[:, PACK * N * h : PACK * N * (h + 1)].bitcast(I32),
                in_=y_codes[:].bitcast(I32),
            )

        head = [samples(0)] + [queries(j) for j in range(QUERY_TILES_A_HALF)] + [samples(1)]
        first_runs = [
            [samples(2), queries(4)],
            [samples(3), queries(5)],
            [queries(6), queries(7)],
            [samples(4), samples(5)],
        ]
        lone = first_runs[-1][-1][1] + 1
        later_runs = {LONE_RUN_STEP: [samples(lone)]}
        for i, n in enumerate(range(lone + 1, SAMPLE_TILES, 2)):
            later_runs[PACK * (2 + i)] = [samples(m) for m in range(n, min(n + 2, SAMPLE_TILES))]
        run_steps = sorted(later_runs)

        for row_tile in head:
            load(row_tile)
        weight_cols = keep.tile([P, Q // P], BF16)
        nc.sync.dma_start(out=weight_cols[:], in_=query_weight.rearrange("(p c) -> p c", p=P))
        step_bf16 = keep.tile([P, GROUPS, PACK], BF16)
        nc.sync.dma_start(out=step_bf16[:], in_=step.rearrange("(g p t) -> p g t", g=GROUPS, t=PACK))
        for run in first_runs + [later_runs[LONE_RUN_STEP]]:
            for row_tile in run:
                load(row_tile)

        def load_behind(s):
            if s >= 1 and lone + s < SAMPLE_TILES:
                load(samples(lone + s))

        turn(head[0])
        for i in range(1, len(head)):
            turn(head[i])
            quantize(head[i - 1])

        step_cols = keep.tile([P, SAMPLE_TILES], F32)
        weight_rows = keep.tile([P, Q], BF16)
        bank = ps_turn.tile([P, 4, P], F32)
        for i in range(4):
            nc.tensor.transpose(
                bank[:, i, :], weight_cols[:].bitcast(F32)[:, i : i + 1].to_broadcast([P, P]), ident[:]
            )
        nc.vector.tensor_copy(out=step_cols[:], in_=step_bf16[:].rearrange("p g t -> p (g t)"))
        nc.vector.tensor_copy(
            out=weight_rows[:].bitcast(F32).rearrange("p (n i) -> p n i", i=4),
            in_=bank[:].rearrange("p i n -> p n i"),
        )

        sort_pairs(first_runs[0][0], nc.vector.tensor_copy, FIRST_UNIT_SORTED)
        waiting = head[-1:]
        for s in range(PACK):
            grad_matmul(s)
            weigh_grad(s)
            quantize(waiting[0])
            feat_matmul(s)
            finish(s)
            for row_tile in waiting[1:]:
                quantize(row_tile)
            sort_pairs(first_runs[s][1], nc.scalar.copy, FIRST_UNIT_SORTED)
            if s + 1 < PACK:
                sort_pairs(first_runs[s + 1][0], nc.vector.tensor_copy, FIRST_UNIT_SORTED)
            load_behind(s)
            waiting = first_runs[s]
            for row_tile in waiting:
                turn(row_tile)

        grad_matmul(PACK)
        weigh_grad(PACK)
        for s in range(PACK, STEPS):
            unit, t = divmod(s, PACK)
            due = [samples(n) for n in (2 * unit + 2, 2 * unit + 3) if t == 0 and n < SAMPLE_TILES]
            if s + 1 < STEPS:
                grad_matmul(s + 1)
            for row_tile in later_runs.get(s, []):
                turn(row_tile)
            if t == 0 and unit >= 2:
                quantize_unit(unit - 2)
            for row_tile in due[:1]:
                quantize(row_tile)
            feat_matmul(s)
            if s + 1 < STEPS:
                weigh_grad(s + 1)
            else:
                quantize_unit(UNITS - 2)
            for row_tile in due[1:]:
                quantize(row_tile)
            if t == 0:
                round_unit(unit - 1, [(nc.scalar.copy, 0, N)])
            finish(s)
            if s in run_steps[:-1]:
                for row_tile in later_runs[run_steps[run_steps.index(s) + 1]][1:]:
                    sort_pairs(row_tile, nc.scalar.copy, LATER_SORTED)
            load_behind(s)

        round_unit(
            UNITS - 1,
            [(nc.vector.tensor_copy, 0, LAST_VECTOR_COLUMNS), (nc.scalar.copy, LAST_VECTOR_COLUMNS, N)],
        )
        quantize_unit(UNITS - 1)
        for quadrant in range(4):
            nc.scalar.dma_start(
                out=out_2[:, 4 * quadrant : 4 * quadrant + 4, :].bitcast(I32),
                in_=y_scales[32 * quadrant : 32 * quadrant + 16, :].bitcast(I32),
            )
